import numpy as np
import ml_dtypes


def mxq(x, axis, fmt="e4m3"):
    dtype, down = {"e4m3": (ml_dtypes.float8_e4m3fn, 7), "e5m2": (ml_dtypes.float8_e5m2, 14)}[fmt]
    v = np.moveaxis(np.asarray(x, np.float32).astype(ml_dtypes.bfloat16).astype(np.float64), axis, -1)
    blocks = v.reshape(v.shape[:-1] + (-1, 32))
    amax = np.abs(blocks).max(-1, keepdims=True)
    byte = np.maximum(np.where(amax > 0, np.frexp(amax)[1] - 1 + 127, 0) - down, 1)
    scale = np.exp2(byte - 127.0)
    codes = (blocks / scale).astype(np.float32).astype(dtype).astype(np.float64)
    return np.moveaxis((codes * scale).reshape(v.shape), -1, axis)


WIDE = False


def mx_kscale(k):
    if not WIDE:
        return np.ones(k)
    levels = np.array([10, -10, 5, -5, 0])
    if k % 512:
        return np.exp2(np.random.permutation(np.resize(levels, k // 32))).repeat(32)
    a = np.empty((k // 512, 16))
    for p in range(k // 512):
        a[p, :8] = np.random.permutation(np.resize(levels, 8))
        for g in range(8):
            far = levels[np.abs(levels - a[p, g]) >= 10]
            a[p, g + 8] = far[np.random.randint(len(far))]
    return np.exp2(a.ravel()).repeat(32)


BF16 = ml_dtypes.bfloat16


def bf(x):
    return np.asarray(x, np.float32).astype(BF16)


def f64(x):
    return np.asarray(x).astype(np.float64)


T, D, F, R = 8192, 256, 1024, 512


def draw0():
    s, t = mx_kscale(F), mx_kscale(T)
    return {
        "x": bf(np.random.standard_normal((T, D)) / t[:, None]),
        "g": bf(np.random.standard_normal((T, F)) * s[None, :] * t[:, None]),
        "p": bf(np.random.standard_normal((D, R))),
        "lam": bf(np.random.uniform(0.5, 1.5, R)),
        "q": bf(np.random.standard_normal((R, F)) / np.sqrt(F) / s[None, :]),
        "avg_i": bf(np.random.uniform(0.2, 1.2, (D, R))),
        "avg_u": bf(np.random.uniform(0.2, 1.2, (D, R))),
    }


def factor_grad(x, g, lam, q):
    u = mxq(g, 1, "e4m3") @ mxq(q, 1, "e4m3").T
    ul = u * lam[None, :]
    return (mxq(x, 0, "e4m3").T @ mxq(ul, 0, "e4m3")) / np.sqrt(T)


def core(x, g, p, lam, q, avg_i, avg_u):
    grad = factor_grad(f64(x), f64(g), f64(lam), f64(q))
    s = np.abs(f64(p) * grad)
    i_new = 0.7 * f64(avg_i) + 0.3 * s
    u_new = 0.7 * f64(avg_u) + 0.3 * np.abs(s - i_new)
    return i_new * u_new


def e4m3fn_bytes(y):
    return np.clip(np.asarray(y, np.float64), -448.0, 448.0).astype(np.float32).astype(ml_dtypes.float8_e4m3fn).view(np.uint8)


def e4m3fn_values(b):
    return np.asarray(b, np.uint8).view(ml_dtypes.float8_e4m3fn).astype(np.float64)


def setup_inputs():
    d = draw0()
    x0 = np.asarray(d['x']).astype(np.float64)
    s = (np.max(np.abs(x0), axis=(1,), keepdims=True) / 448.0).astype(np.float32)
    out = {}
    for k, v in d.items():
        if k == 'x':
            out['x_bytes'] = e4m3fn_bytes(x0 / s.astype(np.float64))
            out['x_scale'] = s
        else:
            out[k] = v
    return out


def reference(x_bytes, x_scale, g, p, lam, q, avg_i, avg_u):
    return core(e4m3fn_values(x_bytes) * x_scale.astype(np.float64), g, p, lam, q, avg_i, avg_u)

@@ -1,0 +1,270 @@
+from contextlib import ExitStack
+
+import concourse.mybir as mybir
+from concourse.masks import make_identity
+
+T, D, F, R = 8192, 256, 1024, 512
+FLOPS = 2 * T * F * R + 2 * T * D * R
+
+F32 = mybir.dt.float32
+BF16 = mybir.dt.bfloat16
+U32 = mybir.dt.uint32
+U8 = mybir.dt.uint8
+F8 = mybir.dt.float8_e4m3fn
+FP8X4 = mybir.dt.float8_e4m3fn_x4
+ALU = mybir.AluOpType
+ACT = mybir.ActivationFunctionType
+
+P = 128
+G = T // 512
+RC = R // 128
+GRAD = 0.3 / 8192**0.5
+
+
+def tile_adalorasensitivityscore_t_kernel(tc, x_bytes, x_scale, g, p, lam, q, avg_i, avg_u, out):
+    nc = tc.nc
+    g_v = g.rearrange("(g p j) f -> g p j f", p=P, j=4)
+    q_v = q.rearrange("(j p) f -> j p f", p=P)
+    xb_v = x_bytes.rearrange("(g p t) n -> p g (t n)", p=P, t=4)
+    xs_v = x_scale.rearrange("(g p t) o -> p g (t o)", p=P, t=4)
+    out_v = out.rearrange("(d p) r -> d p r", p=P)
+
+    with ExitStack() as ctx:
+        const = ctx.enter_context(tc.tile_pool(name="const", bufs=1))
+        graw_pool = ctx.enter_context(tc.tile_pool(name="graw", bufs=5))
+        work = ctx.enter_context(tc.tile_pool(name="work", bufs=2))
+        xbp = ctx.enter_context(tc.tile_pool(name="xbp", bufs=4))
+        acc_pool = ctx.enter_context(tc.psum_pool(name="acc", bufs=1))
+        tp_pool = ctx.enter_context(tc.psum_pool(name="tp", bufs=3))
+        up_pool = ctx.enter_context(tc.psum_pool(name="up", bufs=3))
+        ctx.enter_context(tc.manual_schedule())
+
+        ident = const.tile([P, P], F32, name="ident")
+        ones = const.tile([P, P], BF16, name="ones")
+        lam_row = const.tile([P, R], BF16, name="lam_row")
+        lam_t = const.tile([P, R], F32, name="lam_t")
+        warm = const.tile([P, 2], F32, name="warm")
+        nc.gpsimd.memset(lam_row[:], 0.0)
+        nc.gpsimd.memset(ones[:], 1.0)
+        make_identity(nc, ident[:])
+        nc.vector.memset(warm[:], 1.0)
+        nc.scalar.dma_start(out=lam_row[0:1, :], in_=lam.unsqueeze(0))
+        nc.scalar.activation(out=warm[:, 0:1], in_=warm[:, 1:2], func=ACT.Abs)
+
+        q_raw = const.tile([P, 4, F], BF16, name="q_raw", align_bytes=64)
+        for j in range(4):
+            nc.sync.dma_start(out=q_raw[:, j, :], in_=q_v[j])
+        graw = {}
+
+        def load_g(i, pieces):
+            t = graw_pool.tile([P, 4, F], BF16, name="graw_t", align_bytes=64)
+            graw[i] = t
+            n = 4 // pieces
+            for a in range(pieces):
+                js = slice(a * n, (a + 1) * n)
+                nc.sync.dma_start(out=t[:, js, :], in_=g_v[i][:, js, :])
+
+        load_g(0, 4)
+        load_g(1, 2)
+        xb = []
+
+        def load_x(a):
+            t = xbp.tile([P, 4, 1024], U8, name="xb_t")
+            xb.append(t)
+            nc.sync.dma_start(out=t[:], in_=xb_v[:, 4 * a : 4 * a + 4, :])
+
+        load_x(0)
+        xs = const.tile([P, G, 8], F32, name="xs")
+        nc.sync.dma_start(out=xs[:, :, 0:4], in_=xs_v)
+        load_g(2, 1)
+        load_g(3, 1)
+        load_x(1)
+        load_g(4, 1)
+
+        def transposes(raw, j, bank):
+            words = raw[:, j, :].bitcast(F32)
+            for c in range(2):
+                for u in range(2):
+                    nc.tensor.transpose(bank[:, c, u, :], words[:, 256 * c + u : 256 * (c + 1) : 2], ident[:])
+
+        def drain(eng, bank, grouped, j):
+            dst = grouped[:, j, :].bitcast(F32).rearrange("p (c r u) -> p c r u", c=2, u=2)
+            src = bank[:].rearrange("p c u r -> p c r u")
+            if eng == "v":
+                nc.vector.tensor_copy(out=dst, in_=src)
+            else:
+                nc.scalar.copy(out=dst, in_=src)
+
+        def quantize(grouped, codes, scales, lo, hi):
+            nc.vector.quantize_mx(out=codes[:, lo:hi].bitcast(FP8X4), scales=scales[:, lo:hi], in_=grouped[:, 4 * lo : 4 * hi])
+
+        gq, gc, gs = {}, {}, {}
+
+        def new_g(i):
+            t = work.tile([P, 4, F], BF16, name="gq_t", align_bytes=64)
+            gq[i] = t
+
+        def quant_g(i):
+            c = work.tile([P, 1024], U32, name="gc_t", align_bytes=64)
+            s = work.tile([P, 1024], U8, name="gs_t", align_bytes=64)
+            gc[i], gs[i] = c, s
+            flat = gq[i][:].rearrange("p j f -> p (j f)")
+            quantize(flat, c, s, 0, 512)
+            quantize(flat, c, s, 512, 1024)
+
+        xp, xi, xc, xsc = {}, {}, {}, {}
+
+        def widen_x(i):
+            t = work.tile([P, 4, D], BF16, name="xp_t", align_bytes=64)
+            xp[i] = t
+            src = xb[i // 4]
+            for k in range(4):
+                nc.scalar.activation(
+                    out=t[:, k, :], in_=src[:, i % 4, k * D : (k + 1) * D].bitcast(F8), func=ACT.Copy, scale=xs[:, i, k : k + 1]
+                )
+
+        def interleave_x(i):
+            t = work.tile([P, D, 4], BF16, name="xi_t", align_bytes=64)
+            xi[i] = t
+            nc.scalar.copy(out=t[:], in_=xp[i][:].rearrange("p t n -> p n t"))
+
+        def quant_x(i):
+            c = work.tile([P, D], U32, name="xc_t", align_bytes=64)
+            s = work.tile([P, D], U8, name="xsc_t", align_bytes=64)
+            xc[i], xsc[i] = c, s
+            quantize(xi[i][:].rearrange("p n t -> p (n t)"), c, s, 0, D)
+
+        ul, uc, us = {}, {}, {}
+
+        def mm1(i):
+            u = work.tile([P, R, 4], BF16, name="ul_t", align_bytes=64)
+            ul[i] = u
+            c4 = gc[i][:].rearrange("p (j c r) -> p j c r", j=4, c=2)
+            s4 = gs[i][:].rearrange("p (j c r) -> p j c r", j=4, c=2)
+            for rc in range(RC):
+                ub = up_pool.tile([P, 4, P], F32, name="ub_t")
+                for j in range(4):
+                    for c in range(2):
+                        nc.tensor.matmul_mx(
+                            out=ub[:, j, :],
+                            lhsT=c4[:, j, c, :].bitcast(FP8X4),
+                            lhsT_scale=s4[:, j, c, :],
+                            rhs=qc4[:, rc, c, :].bitcast(FP8X4),
+                            rhs_scale=qs4[:, rc, c, :],
+                            start=(c == 0),
+                            stop=(c == 1),
+                        )
+                cols = slice(rc * P, (rc + 1) * P)
+                nc.vector.tensor_tensor(
+                    out=u[:, cols, :],
+                    in0=ub[:].rearrange("p j n -> p n j"),
+                    in1=lam_t[:, cols].unsqueeze(2).to_broadcast([P, P, 4]),
+                    op=ALU.mult,
+                )
+
+        def quant_u(i):
+            c = work.tile([P, R], U32, name="uc_t", align_bytes=64)
+            s = work.tile([P, R], U8, name="us_t", align_bytes=64)
+            uc[i], us[i] = c, s
+            quantize(ul[i][:].rearrange("p n t -> p (n t)"), c, s, 0, R)
+
+        acc = [acc_pool.tile([P, R], F32, name="acc0"), acc_pool.tile([P, R], F32, name="acc1")]
+
+        def mm2(i):
+            for d in range(2):
+                cols = slice(d * P, (d + 1) * P)
+                nc.tensor.matmul_mx(
+                    out=acc[d][:],
+                    lhsT=xc[i][:, cols].bitcast(FP8X4),
+                    lhsT_scale=xsc[i][:, cols],
+                    rhs=uc[i][:].bitcast(FP8X4),
+                    rhs_scale=us[i][:],
+                    start=(i == 0),
+                    stop=(i == G - 1),
+                )
+
+        lb = up_pool.tile([P, R], F32, name="ub_t")
+        nc.tensor.matmul(lb[:], lhsT=ones[:], rhs=lam_row[:], start=True, stop=True)
+        nc.scalar.copy(out=lam_t[:], in_=lb[:])
+
+        qg = const.tile([P, 4, F], BF16, name="qg", align_bytes=64)
+        q_codes = const.tile([P, 1024], U32, name="q_codes", align_bytes=64)
+        q_scales = const.tile([P, 1024], U8, name="q_scales", align_bytes=64)
+        qc4 = q_codes[:].rearrange("p (j c r) -> p j c r", j=4, c=2)
+        qs4 = q_scales[:].rearrange("p (j c r) -> p j c r", j=4, c=2)
+        q_flat = qg[:].rearrange("p j f -> p (j f)")
+        new_g(0)
+
+        def head_tile(raw, grouped, j, eng):
+            bank = tp_pool.tile([P, 2, 2, P], F32, name="tp_t")
+            transposes(raw, j, bank)
+            drain(eng, bank, grouped, j)
+
+        for j in range(4):
+            head_tile(q_raw, qg, j, "vs"[j % 2])
+        quantize(q_flat, q_codes, q_scales, 0, 512)
+        head_tile(graw[0], gq[0], 0, "s")
+        head_tile(graw[0], gq[0], 1, "v")
+        quantize(q_flat, q_codes, q_scales, 512, 1024)
+        head_tile(graw[0], gq[0], 2, "s")
+        head_tile(graw[0], gq[0], 3, "v")
+        widen_x(0)
+        widen_x(1)
+        interleave_x(0)
+
+        for i in range(G):
+            quant_g(i)
+            if i > 0:
+                quant_u(i - 1)
+            quant_x(i)
+            if i + 1 < G:
+                new_g(i + 1)
+                for j in range(4):
+                    head_tile(graw[i + 1], gq[i + 1], j, "s")
+                interleave_x(i + 1)
+            if i + 2 < G:
+                widen_x(i + 2)
+            mm1(i)
+            if i > 0:
+                mm2(i - 1)
+            if i + 5 < G:
+                load_g(i + 5, 1)
+            if i == 0 or i == 4:
+                load_x(2 + i // 4)
+            if i == 7:
+                p_t = const.tile([P, 2, R], BF16, name="p_t")
+                ai_t = const.tile([P, 2, R], BF16, name="ai_t")
+                au_t = const.tile([P, 2, R], BF16, name="au_t")
+                for dst, src in ((p_t, p), (ai_t, avg_i), (au_t, avg_u)):
+                    nc.sync.dma_start(out=dst[:], in_=src.rearrange("(d p) r -> p d r", p=P))
+
+        quant_u(G - 1)
+        mm2(G - 1)
+
+        H = 256
+        for d in range(2):
+            for h in range(R // H):
+                cols = slice(h * H, (h + 1) * H)
+                y = work.tile([P, H], F32, name="y_t", tag="ep_y", bufs=4)
+                s3 = work.tile([P, H], F32, name="s3_t", tag="ep_s", bufs=4)
+                w = work.tile([P, H], F32, name="w_t", tag="ep_w", bufs=4)
+                aw = work.tile([P, H], F32, name="aw_t", tag="ep_aw", bufs=4)
+                iv = work.tile([P, H], F32, name="iv_t", tag="ep_i", bufs=4)
+                uv = work.tile([P, H], F32, name="uv_t", tag="ep_u", bufs=4)
+                o = work.tile([P, H], F32, name="o_t", tag="ep_o", bufs=4)
+                nc.vector.scalar_tensor_tensor(
+                    out=y[:], in0=acc[d][:, cols], scalar=GRAD, in1=p_t[:, d, cols], op0=ALU.mult, op1=ALU.mult
+                )
+                nc.scalar.activation(out=s3[:], in_=y[:], func=ACT.Abs)
+                nc.vector.scalar_tensor_tensor(
+                    out=w[:], in0=ai_t[:, d, cols], scalar=-0.3, in1=s3[:], op0=ALU.mult, op1=ALU.add
+                )
+                nc.scalar.activation(out=aw[:], in_=w[:], func=ACT.Abs)
+                nc.vector.scalar_tensor_tensor(
+                    out=iv[:], in0=ai_t[:, d, cols], scalar=0.7, in1=s3[:], op0=ALU.mult, op1=ALU.add
+                )
+                nc.vector.tensor_tensor(out=uv[:], in0=au_t[:, d, cols], in1=aw[:], op=ALU.add)
+                nc.vector.scalar_tensor_tensor(
+                    out=o[:], in0=iv[:], scalar=0.7, in1=uv[:], op0=ALU.mult, op1=ALU.mult
+                )
+                nc.sync.dma_start(out=out_v[d][:, cols], in_=o[:])

@@ -104,13 +104,14 @@ def tile_adalorasensitivityscore_t_kernel(tc, x_bytes, x_scale, g, p, lam, q, av
             t = work.tile([P, 4, F], BF16, name="gq_t", align_bytes=64)
             gq[i] = t
 
-        def quant_g(i):
+        def quant_g(i, half):
+            if half == 1:
+                quantize(gq[i][:].rearrange("p j f -> p (j f)"), gc[i], gs[i], 512, 1024)
+                return
             c = work.tile([P, 1024], U32, name="gc_t", align_bytes=64)
             s = work.tile([P, 1024], U8, name="gs_t", align_bytes=64)
             gc[i], gs[i] = c, s
-            flat = gq[i][:].rearrange("p j f -> p (j f)")
-            quantize(flat, c, s, 0, 512)
-            quantize(flat, c, s, 512, 1024)
+            quantize(gq[i][:].rearrange("p j f -> p (j f)"), c, s, 0, 512)
 
         xp, xi, xc, xsc = {}, {}, {}, {}
 
@@ -124,9 +125,11 @@ def tile_adalorasensitivityscore_t_kernel(tc, x_bytes, x_scale, g, p, lam, q, av
                 )
 
         def interleave_x(i):
-            t = work.tile([P, D, 4], BF16, name="xi_t", align_bytes=64)
+            t = const.tile([P, D, 4], BF16, name="xi_t", align_bytes=64)
             xi[i] = t
-            nc.scalar.copy(out=t[:], in_=xp[i][:].rearrange("p t n -> p n t"))
+            nc.gpsimd.tensor_scalar(
+                out=t[:], in0=xp[i][:].rearrange("p t n -> p n t"), scalar1=1.0, scalar2=0.0, op0=ALU.mult, op1=ALU.add
+            )
 
         def quant_x(i):
             c = work.tile([P, D], U32, name="xc_t", align_bytes=64)
@@ -136,12 +139,18 @@ def tile_adalorasensitivityscore_t_kernel(tc, x_bytes, x_scale, g, p, lam, q, av
 
         ul, uc, us = {}, {}, {}
 
-        def mm1(i):
-            u = work.tile([P, R, 4], BF16, name="ul_t", align_bytes=64)
-            ul[i] = u
+        def new_u(i):
+            t = work.tile([P, R, 4], BF16, name="ul_t", align_bytes=64)
+            ul[i] = t
+            c = work.tile([P, R], U32, name="uc_t", align_bytes=64)
+            s = work.tile([P, R], U8, name="us_t", align_bytes=64)
+            uc[i], us[i] = c, s
+
+        def mm1(i, rcs):
+            u = ul[i]
             c4 = gc[i][:].rearrange("p (j c r) -> p j c r", j=4, c=2)
             s4 = gs[i][:].rearrange("p (j c r) -> p j c r", j=4, c=2)
-            for rc in range(RC):
+            for rc in rcs:
                 ub = up_pool.tile([P, 4, P], F32, name="ub_t")
                 for j in range(4):
                     for c in range(2):
@@ -162,11 +171,8 @@ def tile_adalorasensitivityscore_t_kernel(tc, x_bytes, x_scale, g, p, lam, q, av
                     op=ALU.mult,
                 )
 
-        def quant_u(i):
-            c = work.tile([P, R], U32, name="uc_t", align_bytes=64)
-            s = work.tile([P, R], U8, name="us_t", align_bytes=64)
-            uc[i], us[i] = c, s
-            quantize(ul[i][:].rearrange("p n t -> p (n t)"), c, s, 0, R)
+        def quant_u(i, lo, hi):
+            quantize(ul[i][:].rearrange("p n t -> p (n t)"), uc[i], us[i], lo, hi)
 
         acc = [acc_pool.tile([P, R], F32, name="acc0"), acc_pool.tile([P, R], F32, name="acc1")]
 
@@ -208,25 +214,40 @@ def tile_adalorasensitivityscore_t_kernel(tc, x_bytes, x_scale, g, p, lam, q, av
         quantize(q_flat, q_codes, q_scales, 512, 1024)
         head_tile(graw[0], gq[0], 2, "s")
         head_tile(graw[0], gq[0], 3, "v")
+        quant_g(0, 0)
         widen_x(0)
         widen_x(1)
+        quant_g(0, 1)
         interleave_x(0)
 
         for i in range(G):
-            quant_g(i)
-            if i > 0:
-                quant_u(i - 1)
             quant_x(i)
+            new_u(i)
             if i + 1 < G:
-                new_g(i + 1)
-                for j in range(4):
-                    head_tile(graw[i + 1], gq[i + 1], j, "s")
                 interleave_x(i + 1)
+                new_g(i + 1)
+                for j in (0, 1):
+                    head_tile(graw[i + 1], gq[i + 1], j, "s")
+            mm1(i, (0, 1))
+            if i + 1 < G:
+                quant_g(i + 1, 0)
+            if i > 0:
+                quant_u(i - 1, 0, R)
+            if i + 1 < G:
+                for j in (2, 3):
+                    head_tile(graw[i + 1], gq[i + 1], j, "s")
             if i + 2 < G:
                 widen_x(i + 2)
-            mm1(i)
+            if i + 1 < G:
+                mm1(i, (2, 3))
+            else:
+                mm1(i, (2,))
+                quant_u(i, 0, 256)
+                mm1(i, (3,))
             if i > 0:
                 mm2(i - 1)
+            if i + 1 < G:
+                quant_g(i + 1, 1)
             if i + 5 < G:
                 load_g(i + 5, 1)
             if i == 0 or i == 4:
@@ -238,33 +259,49 @@ def tile_adalorasensitivityscore_t_kernel(tc, x_bytes, x_scale, g, p, lam, q, av
                 for dst, src in ((p_t, p), (ai_t, avg_i), (au_t, avg_u)):
                     nc.sync.dma_start(out=dst[:], in_=src.rearrange("(d p) r -> p d r", p=P))
 
-        quant_u(G - 1)
+        quant_u(G - 1, 256, R)
         mm2(G - 1)
 
         H = 256
-        for d in range(2):
-            for h in range(R // H):
-                cols = slice(h * H, (h + 1) * H)
-                y = work.tile([P, H], F32, name="y_t", tag="ep_y", bufs=4)
-                s3 = work.tile([P, H], F32, name="s3_t", tag="ep_s", bufs=4)
-                w = work.tile([P, H], F32, name="w_t", tag="ep_w", bufs=4)
-                aw = work.tile([P, H], F32, name="aw_t", tag="ep_aw", bufs=4)
-                iv = work.tile([P, H], F32, name="iv_t", tag="ep_i", bufs=4)
-                uv = work.tile([P, H], F32, name="uv_t", tag="ep_u", bufs=4)
-                o = work.tile([P, H], F32, name="o_t", tag="ep_o", bufs=4)
-                nc.vector.scalar_tensor_tensor(
-                    out=y[:], in0=acc[d][:, cols], scalar=GRAD, in1=p_t[:, d, cols], op0=ALU.mult, op1=ALU.mult
-                )
-                nc.scalar.activation(out=s3[:], in_=y[:], func=ACT.Abs)
-                nc.vector.scalar_tensor_tensor(
-                    out=w[:], in0=ai_t[:, d, cols], scalar=-0.3, in1=s3[:], op0=ALU.mult, op1=ALU.add
-                )
-                nc.scalar.activation(out=aw[:], in_=w[:], func=ACT.Abs)
-                nc.vector.scalar_tensor_tensor(
-                    out=iv[:], in0=ai_t[:, d, cols], scalar=0.7, in1=s3[:], op0=ALU.mult, op1=ALU.add
-                )
-                nc.vector.tensor_tensor(out=uv[:], in0=au_t[:, d, cols], in1=aw[:], op=ALU.add)
-                nc.vector.scalar_tensor_tensor(
-                    out=o[:], in0=iv[:], scalar=0.7, in1=uv[:], op0=ALU.mult, op1=ALU.mult
-                )
-                nc.sync.dma_start(out=out_v[d][:, cols], in_=o[:])
+        chunks = [(d, slice(h * H, (h + 1) * H)) for d in range(2) for h in range(R // H)]
+        ys, ss, ws, aws, ivs, uvs, os_ = {}, {}, {}, {}, {}, {}, {}
+
+        def ep_tile(store, k, nm):
+            t = work.tile([P, H], F32, name=nm, bufs=4)
+            store[k] = t
+            return t[:]
+
+        def ep_y(k):
+            d, cols = chunks[k]
+            nc.vector.scalar_tensor_tensor(
+                out=ep_tile(ys, k, "y_t"), in0=acc[d][:, cols], scalar=GRAD, in1=p_t[:, d, cols], op0=ALU.mult, op1=ALU.mult
+            )
+            nc.scalar.activation(out=ep_tile(ss, k, "s3_t"), in_=ys[k][:], func=ACT.Abs)
+
+        def ep_w(k):
+            d, cols = chunks[k]
+            nc.vector.scalar_tensor_tensor(
+                out=ep_tile(ws, k, "w_t"), in0=ai_t[:, d, cols], scalar=-0.3, in1=ss[k][:], op0=ALU.mult, op1=ALU.add
+            )
+            nc.scalar.activation(out=ep_tile(aws, k, "aw_t"), in_=ws[k][:], func=ACT.Abs)
+
+        def ep_i(k):
+            d, cols = chunks[k]
+            nc.vector.scalar_tensor_tensor(
+                out=ep_tile(ivs, k, "iv_t"), in0=ai_t[:, d, cols], scalar=0.7, in1=ss[k][:], op0=ALU.mult, op1=ALU.add
+            )
+
+        def ep_u(k):
+            d, cols = chunks[k]
+            nc.vector.tensor_tensor(out=ep_tile(uvs, k, "uv_t"), in0=au_t[:, d, cols], in1=aws[k][:], op=ALU.add)
+
+        def ep_o(k):
+            d, cols = chunks[k]
+            nc.vector.scalar_tensor_tensor(
+                out=ep_tile(os_, k, "o_t"), in0=ivs[k][:], scalar=0.7, in1=uvs[k][:], op0=ALU.mult, op1=ALU.mult
+            )
+            nc.sync.dma_start(out=out_v[d][:, cols], in_=os_[k][:])
+
+        for step in ((ep_y, 0), (ep_y, 1), (ep_w, 0), (ep_y, 2), (ep_w, 1), (ep_i, 0), (ep_y, 3), (ep_u, 0), (ep_i, 1), (ep_w, 2),
+                     (ep_o, 0), (ep_u, 1), (ep_w, 3), (ep_i, 2), (ep_o, 1), (ep_u, 2), (ep_i, 3), (ep_o, 2), (ep_u, 3), (ep_o, 3)):
+            step[0](step[1])

@@ -65,7 +65,8 @@ def tile_adalorasensitivityscore_t_kernel(tc, x_bytes, x_scale, g, p, lam, q, av
                 nc.sync.dma_start(out=t[:, js, :], in_=g_v[i][:, js, :])
 
         load_g(0, 4)
-        load_g(1, 2)
+        load_g(1, 4)
+        load_g(2, 2)
         xb = []
 
         def load_x(a):
@@ -73,19 +74,29 @@ def tile_adalorasensitivityscore_t_kernel(tc, x_bytes, x_scale, g, p, lam, q, av
             xb.append(t)
             nc.sync.dma_start(out=t[:], in_=xb_v[:, 4 * a : 4 * a + 4, :])
 
-        load_x(0)
         xs = const.tile([P, G, 8], F32, name="xs")
         nc.sync.dma_start(out=xs[:, :, 0:4], in_=xs_v)
-        load_g(2, 1)
+        load_x(0)
         load_g(3, 1)
         load_x(1)
         load_g(4, 1)
 
-        def transposes(raw, j, bank):
+        pre = {}
+
+        def preorder(i, j):
+            t = work.tile([P, 2, 2, P], F32, name="pre_t", align_bytes=64, bufs=4)
+            pre[i, j] = t
+            nc.scalar.copy(out=t[:], in_=graw[i][:, j, :].bitcast(F32).rearrange("p (c r u) -> p c u r", c=2, u=2))
+
+        def transposes(raw, j, bank, key=None):
             words = raw[:, j, :].bitcast(F32)
             for c in range(2):
                 for u in range(2):
-                    nc.tensor.transpose(bank[:, c, u, :], words[:, 256 * c + u : 256 * (c + 1) : 2], ident[:])
+                    if key in pre:
+                        src = pre[key][:, c, u, :]
+                    else:
+                        src = words[:, 256 * c + u : 256 * (c + 1) : 2]
+                    nc.tensor.transpose(bank[:, c, u, :], src, ident[:])
 
         def drain(eng, bank, grouped, j):
             dst = grouped[:, j, :].bitcast(F32).rearrange("p (c r u) -> p c r u", c=2, u=2)
@@ -116,7 +127,7 @@ def tile_adalorasensitivityscore_t_kernel(tc, x_bytes, x_scale, g, p, lam, q, av
         xp, xi, xc, xsc = {}, {}, {}, {}
 
         def widen_x(i):
-            t = work.tile([P, 4, D], BF16, name="xp_t", align_bytes=64)
+            t = work.tile([P, 4, D], BF16, name="xp_t", align_bytes=64, bufs=4)
             xp[i] = t
             src = xb[i // 4]
             for k in range(4):
@@ -132,8 +143,8 @@ def tile_adalorasensitivityscore_t_kernel(tc, x_bytes, x_scale, g, p, lam, q, av
             )
 
         def quant_x(i):
-            c = work.tile([P, D], U32, name="xc_t", align_bytes=64)
-            s = work.tile([P, D], U8, name="xsc_t", align_bytes=64)
+            c = work.tile([P, D], U32, name="xc_t", align_bytes=64, bufs=4)
+            s = work.tile([P, D], U8, name="xsc_t", align_bytes=64, bufs=4)
             xc[i], xsc[i] = c, s
             quantize(xi[i][:].rearrange("p n t -> p (n t)"), c, s, 0, D)
 
@@ -142,8 +153,8 @@ def tile_adalorasensitivityscore_t_kernel(tc, x_bytes, x_scale, g, p, lam, q, av
         def new_u(i):
             t = work.tile([P, R, 4], BF16, name="ul_t", align_bytes=64)
             ul[i] = t
-            c = work.tile([P, R], U32, name="uc_t", align_bytes=64)
-            s = work.tile([P, R], U8, name="us_t", align_bytes=64)
+            c = work.tile([P, R], U32, name="uc_t", align_bytes=64, bufs=4)
+            s = work.tile([P, R], U8, name="us_t", align_bytes=64, bufs=4)
             uc[i], us[i] = c, s
 
         def mm1(i, rcs):
@@ -189,10 +200,6 @@ def tile_adalorasensitivityscore_t_kernel(tc, x_bytes, x_scale, g, p, lam, q, av
                     stop=(i == G - 1),
                 )
 
-        lb = up_pool.tile([P, R], F32, name="ub_t")
-        nc.tensor.matmul(lb[:], lhsT=ones[:], rhs=lam_row[:], start=True, stop=True)
-        nc.scalar.copy(out=lam_t[:], in_=lb[:])
-
         qg = const.tile([P, 4, F], BF16, name="qg", align_bytes=64)
         q_codes = const.tile([P, 1024], U32, name="q_codes", align_bytes=64)
         q_scales = const.tile([P, 1024], U8, name="q_scales", align_bytes=64)
@@ -201,9 +208,9 @@ def tile_adalorasensitivityscore_t_kernel(tc, x_bytes, x_scale, g, p, lam, q, av
         q_flat = qg[:].rearrange("p j f -> p (j f)")
         new_g(0)
 
-        def head_tile(raw, grouped, j, eng):
+        def head_tile(raw, grouped, j, eng, key=None):
             bank = tp_pool.tile([P, 2, 2, P], F32, name="tp_t")
-            transposes(raw, j, bank)
+            transposes(raw, j, bank, key)
             drain(eng, bank, grouped, j)
 
         for j in range(4):
@@ -215,43 +222,63 @@ def tile_adalorasensitivityscore_t_kernel(tc, x_bytes, x_scale, g, p, lam, q, av
         head_tile(graw[0], gq[0], 2, "s")
         head_tile(graw[0], gq[0], 3, "v")
         quant_g(0, 0)
-        widen_x(0)
-        widen_x(1)
         quant_g(0, 1)
-        interleave_x(0)
+        new_g(1)
+        for j in range(4):
+            head_tile(graw[1], gq[1], j, "s")
+        lb = up_pool.tile([P, R], F32, name="ub_t")
+        nc.tensor.matmul(lb[:], lhsT=ones[:], rhs=lam_row[:], start=True, stop=True)
+        nc.scalar.copy(out=lam_t[:], in_=lb[:])
+        preorder(2, 0)
+        preorder(2, 2)
+
+        widen_at = {1: (0, 1), 2: (2, 3), **{i: (i + 1,) for i in range(3, G - 1)}}
+        x_start = {2: (None, 0), 3: (1, 2), **{i: (i - 1, i) for i in range(4, G)}}
+        x_mid = {2: (0, 1), 3: (2, 3)}
+        mm2_at = {2: (0,), 3: (1, 2), **{i: (i - 1,) for i in range(4, G)}}
+
+        def x_turn(turn):
+            done, following = turn
+            if done is not None:
+                quant_x(done)
+            if following is not None:
+                interleave_x(following)
 
         for i in range(G):
-            quant_x(i)
+            lead = 0 < i < G - 1
+            x_turn(x_start.get(i, (None, None)))
             new_u(i)
-            if i + 1 < G:
-                interleave_x(i + 1)
+            if lead:
                 new_g(i + 1)
                 for j in (0, 1):
-                    head_tile(graw[i + 1], gq[i + 1], j, "s")
+                    head_tile(graw[i + 1], gq[i + 1], j, "s", (i + 1, j))
             mm1(i, (0, 1))
             if i + 1 < G:
                 quant_g(i + 1, 0)
             if i > 0:
                 quant_u(i - 1, 0, R)
-            if i + 1 < G:
+            x_turn(x_mid.get(i, (None, None)))
+            if lead:
                 for j in (2, 3):
-                    head_tile(graw[i + 1], gq[i + 1], j, "s")
-            if i + 2 < G:
-                widen_x(i + 2)
-            if i + 1 < G:
-                mm1(i, (2, 3))
-            else:
-                mm1(i, (2,))
-                quant_u(i, 0, 256)
-                mm1(i, (3,))
-            if i > 0:
-                mm2(i - 1)
+                    head_tile(graw[i + 1], gq[i + 1], j, "s", (i + 1, j))
+            if 0 < i < G - 2:
+                preorder(i + 2, 0)
+                preorder(i + 2, 2)
+            for k in widen_at.get(i, ()):
+                widen_x(k)
+            mm1(i, (2,))
             if i + 1 < G:
                 quant_g(i + 1, 1)
+            else:
+                quant_x(i)
+                quant_u(i, 0, 256)
+            mm1(i, (3,))
+            for k in mm2_at.get(i, ()):
+                mm2(k)
             if i + 5 < G:
                 load_g(i + 5, 1)
-            if i == 0 or i == 4:
-                load_x(2 + i // 4)
+            if i == 2 or i == 6:
+                load_x(2 + i // 6)
             if i == 7:
                 p_t = const.tile([P, 2, R], BF16, name="p_t")
                 ai_t = const.tile([P, 2, R], BF16, name="ai_t")

from contextlib import ExitStack

import concourse.mybir as mybir
from concourse.masks import make_identity

T, D, F, R = 8192, 256, 1024, 512
FLOPS = 2 * T * F * R + 2 * T * D * R

F32 = mybir.dt.float32
BF16 = mybir.dt.bfloat16
U32 = mybir.dt.uint32
U8 = mybir.dt.uint8
F8 = mybir.dt.float8_e4m3fn
FP8X4 = mybir.dt.float8_e4m3fn_x4
ALU = mybir.AluOpType
ACT = mybir.ActivationFunctionType

P = 128
G = T // 512
RC = R // 128
GRAD = 0.3 / 8192**0.5


def tile_adalorasensitivityscore_t_kernel(tc, x_bytes, x_scale, g, p, lam, q, avg_i, avg_u, out):
    nc = tc.nc
    g_v = g.rearrange("(g p j) f -> g p j f", p=P, j=4)
    q_v = q.rearrange("(j p) f -> j p f", p=P)
    xb_v = x_bytes.rearrange("(g p t) n -> p g (t n)", p=P, t=4)
    xs_v = x_scale.rearrange("(g p t) o -> p g (t o)", p=P, t=4)
    out_v = out.rearrange("(d p) r -> d p r", p=P)

    with ExitStack() as ctx:
        const = ctx.enter_context(tc.tile_pool(name="const", bufs=1))
        graw_pool = ctx.enter_context(tc.tile_pool(name="graw", bufs=5))
        work = ctx.enter_context(tc.tile_pool(name="work", bufs=2))
        xbp = ctx.enter_context(tc.tile_pool(name="xbp", bufs=4))
        acc_pool = ctx.enter_context(tc.psum_pool(name="acc", bufs=1))
        tp_pool = ctx.enter_context(tc.psum_pool(name="tp", bufs=3))
        up_pool = ctx.enter_context(tc.psum_pool(name="up", bufs=3))
        ctx.enter_context(tc.manual_schedule())

        ident = const.tile([P, P], F32, name="ident")
        ones = const.tile([P, P], BF16, name="ones")
        lam_row = const.tile([P, R], BF16, name="lam_row")
        lam_t = const.tile([P, R], F32, name="lam_t")
        warm = const.tile([P, 2], F32, name="warm")
        nc.gpsimd.memset(lam_row[:], 0.0)
        nc.gpsimd.memset(ones[:], 1.0)
        make_identity(nc, ident[:])
        nc.vector.memset(warm[:], 1.0)
        nc.scalar.dma_start(out=lam_row[0:1, :], in_=lam.unsqueeze(0))
        nc.scalar.activation(out=warm[:, 0:1], in_=warm[:, 1:2], func=ACT.Abs)

        q_raw = const.tile([P, 4, F], BF16, name="q_raw", align_bytes=64)
        for j in range(4):
            nc.sync.dma_start(out=q_raw[:, j, :], in_=q_v[j])
        graw = {}

        def load_g(i, pieces):
            t = graw_pool.tile([P, 4, F], BF16, name="graw_t", align_bytes=64)
            graw[i] = t
            n = 4 // pieces
            for a in range(pieces):
                js = slice(a * n, (a + 1) * n)
                nc.sync.dma_start(out=t[:, js, :], in_=g_v[i][:, js, :])

        load_g(0, 4)
        load_g(1, 4)
        load_g(2, 2)
        xb = []

        def load_x(a):
            t = xbp.tile([P, 4, 1024], U8, name="xb_t")
            xb.append(t)
            nc.sync.dma_start(out=t[:], in_=xb_v[:, 4 * a : 4 * a + 4, :])

        xs = const.tile([P, G, 8], F32, name="xs")
        nc.sync.dma_start(out=xs[:, :, 0:4], in_=xs_v)
        load_x(0)
        load_g(3, 1)
        load_x(1)
        load_g(4, 1)

        pre = {}

        def preorder(i, j):
            t = work.tile([P, 2, 2, P], F32, name="pre_t", align_bytes=64, bufs=4)
            pre[i, j] = t
            nc.scalar.copy(out=t[:], in_=graw[i][:, j, :].bitcast(F32).rearrange("p (c r u) -> p c u r", c=2, u=2))

        def transposes(raw, j, bank, key=None):
            words = raw[:, j, :].bitcast(F32)
            for c in range(2):
                for u in range(2):
                    if key in pre:
                        src = pre[key][:, c, u, :]
                    else:
                        src = words[:, 256 * c + u : 256 * (c + 1) : 2]
                    nc.tensor.transpose(bank[:, c, u, :], src, ident[:])

        def drain(eng, bank, grouped, j):
            dst = grouped[:, j, :].bitcast(F32).rearrange("p (c r u) -> p c r u", c=2, u=2)
            src = bank[:].rearrange("p c u r -> p c r u")
            if eng == "v":
                nc.vector.tensor_copy(out=dst, in_=src)
            else:
                nc.scalar.copy(out=dst, in_=src)

        def quantize(grouped, codes, scales, lo, hi):
            nc.vector.quantize_mx(out=codes[:, lo:hi].bitcast(FP8X4), scales=scales[:, lo:hi], in_=grouped[:, 4 * lo : 4 * hi])

        gq, gc, gs = {}, {}, {}

        def new_g(i):
            t = work.tile([P, 4, F], BF16, name="gq_t", align_bytes=64)
            gq[i] = t

        def quant_g(i, half):
            if half == 1:
                quantize(gq[i][:].rearrange("p j f -> p (j f)"), gc[i], gs[i], 512, 1024)
                return
            c = work.tile([P, 1024], U32, name="gc_t", align_bytes=64)
            s = work.tile([P, 1024], U8, name="gs_t", align_bytes=64)
            gc[i], gs[i] = c, s
            quantize(gq[i][:].rearrange("p j f -> p (j f)"), c, s, 0, 512)

        xp, xi, xc, xsc = {}, {}, {}, {}

        def widen_x(i):
            t = work.tile([P, 4, D], BF16, name="xp_t", align_bytes=64, bufs=4)
            xp[i] = t
            src = xb[i // 4]
            for k in range(4):
                nc.scalar.activation(
                    out=t[:, k, :], in_=src[:, i % 4, k * D : (k + 1) * D].bitcast(F8), func=ACT.Copy, scale=xs[:, i, k : k + 1]
                )

        def interleave_x(i):
            t = const.tile([P, D, 4], BF16, name="xi_t", align_bytes=64)
            xi[i] = t
            nc.gpsimd.tensor_scalar(
                out=t[:], in0=xp[i][:].rearrange("p t n -> p n t"), scalar1=1.0, scalar2=0.0, op0=ALU.mult, op1=ALU.add
            )

        def quant_x(i):
            c = work.tile([P, D], U32, name="xc_t", align_bytes=64, bufs=4)
            s = work.tile([P, D], U8, name="xsc_t", align_bytes=64, bufs=4)
            xc[i], xsc[i] = c, s
            quantize(xi[i][:].rearrange("p n t -> p (n t)"), c, s, 0, D)

        ul, uc, us = {}, {}, {}

        def new_u(i):
            t = work.tile([P, R, 4], BF16, name="ul_t", align_bytes=64)
            ul[i] = t
            c = work.tile([P, R], U32, name="uc_t", align_bytes=64, bufs=4)
            s = work.tile([P, R], U8, name="us_t", align_bytes=64, bufs=4)
            uc[i], us[i] = c, s

        def mm1(i, rcs):
            u = ul[i]
            c4 = gc[i][:].rearrange("p (j c r) -> p j c r", j=4, c=2)
            s4 = gs[i][:].rearrange("p (j c r) -> p j c r", j=4, c=2)
            for rc in rcs:
                ub = up_pool.tile([P, 4, P], F32, name="ub_t")
                for j in range(4):
                    for c in range(2):
                        nc.tensor.matmul_mx(
                            out=ub[:, j, :],
                            lhsT=c4[:, j, c, :].bitcast(FP8X4),
                            lhsT_scale=s4[:, j, c, :],
                            rhs=qc4[:, rc, c, :].bitcast(FP8X4),
                            rhs_scale=qs4[:, rc, c, :],
                            start=(c == 0),
                            stop=(c == 1),
                        )
                cols = slice(rc * P, (rc + 1) * P)
                nc.vector.tensor_tensor(
                    out=u[:, cols, :],
                    in0=ub[:].rearrange("p j n -> p n j"),
                    in1=lam_t[:, cols].unsqueeze(2).to_broadcast([P, P, 4]),
                    op=ALU.mult,
                )

        def quant_u(i, lo, hi):
            quantize(ul[i][:].rearrange("p n t -> p (n t)"), uc[i], us[i], lo, hi)

        acc = [acc_pool.tile([P, R], F32, name="acc0"), acc_pool.tile([P, R], F32, name="acc1")]

        def mm2(i):
            for d in range(2):
                cols = slice(d * P, (d + 1) * P)
                nc.tensor.matmul_mx(
                    out=acc[d][:],
                    lhsT=xc[i][:, cols].bitcast(FP8X4),
                    lhsT_scale=xsc[i][:, cols],
                    rhs=uc[i][:].bitcast(FP8X4),
                    rhs_scale=us[i][:],
                    start=(i == 0),
                    stop=(i == G - 1),
                )

        qg = const.tile([P, 4, F], BF16, name="qg", align_bytes=64)
        q_codes = const.tile([P, 1024], U32, name="q_codes", align_bytes=64)
        q_scales = const.tile([P, 1024], U8, name="q_scales", align_bytes=64)
        qc4 = q_codes[:].rearrange("p (j c r) -> p j c r", j=4, c=2)
        qs4 = q_scales[:].rearrange("p (j c r) -> p j c r", j=4, c=2)
        q_flat = qg[:].rearrange("p j f -> p (j f)")
        new_g(0)

        def head_tile(raw, grouped, j, eng, key=None):
            bank = tp_pool.tile([P, 2, 2, P], F32, name="tp_t")
            transposes(raw, j, bank, key)
            drain(eng, bank, grouped, j)

        for j in range(4):
            head_tile(q_raw, qg, j, "vs"[j % 2])
        quantize(q_flat, q_codes, q_scales, 0, 512)
        head_tile(graw[0], gq[0], 0, "s")
        head_tile(graw[0], gq[0], 1, "v")
        quantize(q_flat, q_codes, q_scales, 512, 1024)
        head_tile(graw[0], gq[0], 2, "s")
        head_tile(graw[0], gq[0], 3, "v")
        quant_g(0, 0)
        quant_g(0, 1)
        new_g(1)
        for j in range(4):
            head_tile(graw[1], gq[1], j, "s")
        lb = up_pool.tile([P, R], F32, name="ub_t")
        nc.tensor.matmul(lb[:], lhsT=ones[:], rhs=lam_row[:], start=True, stop=True)
        nc.scalar.copy(out=lam_t[:], in_=lb[:])
        preorder(2, 0)
        preorder(2, 2)

        widen_at = {1: (0, 1), 2: (2, 3), **{i: (i + 1,) for i in range(3, G - 1)}}
        x_start = {2: (None, 0), 3: (1, 2), **{i: (i - 1, i) for i in range(4, G)}}
        x_mid = {2: (0, 1), 3: (2, 3)}
        mm2_at = {2: (0,), 3: (1, 2), **{i: (i - 1,) for i in range(4, G)}}

        def x_turn(turn):
            done, following = turn
            if done is not None:
                quant_x(done)
            if following is not None:
                interleave_x(following)

        for i in range(G):
            lead = 0 < i < G - 1
            x_turn(x_start.get(i, (None, None)))
            new_u(i)
            if lead:
                new_g(i + 1)
                for j in (0, 1):
                    head_tile(graw[i + 1], gq[i + 1], j, "s", (i + 1, j))
            mm1(i, (0, 1))
            if i + 1 < G:
                quant_g(i + 1, 0)
            if i > 0:
                quant_u(i - 1, 0, R)
            x_turn(x_mid.get(i, (None, None)))
            if lead:
                for j in (2, 3):
                    head_tile(graw[i + 1], gq[i + 1], j, "s", (i + 1, j))
            if 0 < i < G - 2:
                preorder(i + 2, 0)
                preorder(i + 2, 2)
            for k in widen_at.get(i, ()):
                widen_x(k)
            mm1(i, (2,))
            if i + 1 < G:
                quant_g(i + 1, 1)
            else:
                quant_x(i)
                quant_u(i, 0, 256)
            mm1(i, (3,))
            for k in mm2_at.get(i, ()):
                mm2(k)
            if i + 5 < G:
                load_g(i + 5, 1)
            if i == 2 or i == 6:
                load_x(2 + i // 6)
            if i == 7:
                p_t = const.tile([P, 2, R], BF16, name="p_t")
                ai_t = const.tile([P, 2, R], BF16, name="ai_t")
                au_t = const.tile([P, 2, R], BF16, name="au_t")
                for dst, src in ((p_t, p), (ai_t, avg_i), (au_t, avg_u)):
                    nc.sync.dma_start(out=dst[:], in_=src.rearrange("(d p) r -> p d r", p=P))

        quant_u(G - 1, 256, R)
        mm2(G - 1)

        H = 256
        chunks = [(d, slice(h * H, (h + 1) * H)) for d in range(2) for h in range(R // H)]
        ys, ss, ws, aws, ivs, uvs, os_ = {}, {}, {}, {}, {}, {}, {}

        def ep_tile(store, k, nm):
            t = work.tile([P, H], F32, name=nm, bufs=4)
            store[k] = t
            return t[:]

        def ep_y(k):
            d, cols = chunks[k]
            nc.vector.scalar_tensor_tensor(
                out=ep_tile(ys, k, "y_t"), in0=acc[d][:, cols], scalar=GRAD, in1=p_t[:, d, cols], op0=ALU.mult, op1=ALU.mult
            )
            nc.scalar.activation(out=ep_tile(ss, k, "s3_t"), in_=ys[k][:], func=ACT.Abs)

        def ep_w(k):
            d, cols = chunks[k]
            nc.vector.scalar_tensor_tensor(
                out=ep_tile(ws, k, "w_t"), in0=ai_t[:, d, cols], scalar=-0.3, in1=ss[k][:], op0=ALU.mult, op1=ALU.add
            )
            nc.scalar.activation(out=ep_tile(aws, k, "aw_t"), in_=ws[k][:], func=ACT.Abs)

        def ep_i(k):
            d, cols = chunks[k]
            nc.vector.scalar_tensor_tensor(
                out=ep_tile(ivs, k, "iv_t"), in0=ai_t[:, d, cols], scalar=0.7, in1=ss[k][:], op0=ALU.mult, op1=ALU.add
            )

        def ep_u(k):
            d, cols = chunks[k]
            nc.vector.tensor_tensor(out=ep_tile(uvs, k, "uv_t"), in0=au_t[:, d, cols], in1=aws[k][:], op=ALU.add)

        def ep_o(k):
            d, cols = chunks[k]
            nc.vector.scalar_tensor_tensor(
                out=ep_tile(os_, k, "o_t"), in0=ivs[k][:], scalar=0.7, in1=uvs[k][:], op0=ALU.mult, op1=ALU.mult
            )
            nc.sync.dma_start(out=out_v[d][:, cols], in_=os_[k][:])

        for step in ((ep_y, 0), (ep_y, 1), (ep_w, 0), (ep_y, 2), (ep_w, 1), (ep_i, 0), (ep_y, 3), (ep_u, 0), (ep_i, 1), (ep_w, 2),
                     (ep_o, 0), (ep_u, 1), (ep_w, 3), (ep_i, 2), (ep_o, 1), (ep_u, 2), (ep_i, 3), (ep_o, 2), (ep_u, 3), (ep_o, 3)):
            step[0](step[1])
